import numpy as np
import ml_dtypes


def mxq(x, axis, fmt="e4m3"):
    dtype, down = {"e4m3": (ml_dtypes.float8_e4m3fn, 7), "e5m2": (ml_dtypes.float8_e5m2, 14)}[fmt]
    v = np.moveaxis(np.asarray(x, np.float32).astype(ml_dtypes.bfloat16).astype(np.float64), axis, -1)
    blocks = v.reshape(v.shape[:-1] + (-1, 32))
    amax = np.abs(blocks).max(-1, keepdims=True)
    byte = np.maximum(np.where(amax > 0, np.frexp(amax)[1] - 1 + 127, 0) - down, 1)
    scale = np.exp2(byte - 127.0)
    codes = (blocks / scale).astype(np.float32).astype(dtype).astype(np.float64)
    return np.moveaxis((codes * scale).reshape(v.shape), -1, axis)


WIDE = False


def mx_kscale(k):
    if not WIDE:
        return np.ones(k)
    levels = np.array([10, -10, 5, -5, 0])
    if k % 512:
        return np.exp2(np.random.permutation(np.resize(levels, k // 32))).repeat(32)
    a = np.empty((k // 512, 16))
    for p in range(k // 512):
        a[p, :8] = np.random.permutation(np.resize(levels, 8))
        for g in range(8):
            far = levels[np.abs(levels - a[p, g]) >= 10]
            a[p, g + 8] = far[np.random.randint(len(far))]
    return np.exp2(a.ravel()).repeat(32)


def f64(x):
    return np.asarray(x).astype(np.float64)


def striped(idx):
    return np.tile(idx.reshape(-1, 16).T, (8, 1)).astype(np.uint16)


def unstriped(offs):
    return offs[:16].T.reshape(-1).astype(np.int64)


E2M1 = np.array([0.0, 0.5, 1.0, 1.5, 2.0, 3.0, 4.0, 6.0, -0.0, -0.5, -1.0, -1.5, -2.0, -3.0, -4.0, -6.0])


def pack_weight(w, fmt):
    k, n = w.shape
    w = f64(np.asarray(w, np.float32).astype(ml_dtypes.bfloat16)).reshape(k // 32, 32, n)
    amax = np.abs(w).max(1)
    if fmt == "e4m3":
        byte = np.frexp(amax)[1] - 1 + 127 - 7
    else:
        mant, ex = np.frexp(amax / 6.0)
        byte = np.where(mant > 0.5, ex, ex - 1) + 127
    byte = np.clip(np.where(amax > 0, byte, 1), 1, 254)
    scaled = (w * np.exp2(127.0 - byte)[:, None, :]).reshape(k, n).astype(np.float32)
    by_word = np.ascontiguousarray(scaled.reshape(k // 512, 128, 4, n).transpose(0, 1, 3, 2))
    if fmt == "e4m3":
        words = by_word.astype(ml_dtypes.float8_e4m3fn).view(np.uint8)
    else:
        c = by_word.astype(ml_dtypes.float4_e2m1fn).view(np.uint8) & 0xF
        words = (c[..., 0::2] | (c[..., 1::2] << 4)).reshape(k // 512, 128, 2 * n)
    return np.ascontiguousarray(words), np.ascontiguousarray(byte.astype(np.uint8).reshape(k // 512, 16, n))


def unpack_weight(words, scales, fmt):
    g, _, n = scales.shape
    words = np.ascontiguousarray(words).reshape(g, 128, n, -1)
    if fmt == "e4m3":
        vals = words.view(ml_dtypes.float8_e4m3fn).astype(np.float64)
    else:
        nib = np.empty((g, 128, n, 4), np.uint8)
        nib[..., 0::2] = words & 0xF
        nib[..., 1::2] = words >> 4
        vals = E2M1[nib]
    vals = vals * np.repeat(np.exp2(scales.astype(np.float64) - 127.0), 8, axis=1)[..., None]
    return vals.transpose(0, 1, 3, 2).reshape(g * 512, n)


def gelu(v):
    return 0.5 * v * (1.0 + np.tanh(np.sqrt(2.0 / np.pi) * (v + 0.044715 * v**3)))


def bf(x):
    return np.asarray(x, np.float32).astype(ml_dtypes.bfloat16)


def planes(Y):
    n, m = Y.shape
    b = f64(bf(Y)).reshape(n // 32, 32, m)
    amax = np.abs(b).max(1)
    byte = np.clip(np.where(amax > 0, np.frexp(amax)[1] - 1 + 127 - 7, 1), 1, 254)
    codes = (b * np.exp2(127.0 - byte)[:, None, :]).reshape(n, m).astype(np.float32).astype(ml_dtypes.float8_e4m3fn).view(np.uint8)
    words = codes.reshape(n // 512, 128, 4, m).transpose(0, 1, 3, 2)
    return np.ascontiguousarray(words), np.ascontiguousarray(byte.astype(np.uint8).reshape(n // 512, 16, m))


K, H, N, T, S, T2, P = 1536, 512, 640, 4096, 1024, 2048, 1024

def setup_inputs():
    n = np.random.standard_normal
    s = mx_kscale(K)[:, None]
    u = mx_kscale(H)[:, None]
    d = {}
    d["tab_words"], d["tab_scales"] = pack_weight(n((K, T)) * s, "e4m3")
    d["offs"] = striped(np.random.permutation(T)[:S])
    d["offs2"] = striped(np.random.permutation(T2)[:S])
    d["offs3"] = striped(np.random.permutation(T2)[:P])
    d["w1"] = (n((K, H)) / K ** 0.5 / s * u.T).astype(np.float32)
    d["w2_words"], d["w2_scales"] = pack_weight(n((K, H)) / K ** 0.5 / s * u.T, "e2m1")
    d["page0"] = (1.2 * np.abs(n((H, T2))) * u).astype(np.float32)
    d["wgs"] = np.exp(0.3 * n((128, S))).astype(np.float32)
    d["ref"] = ((1.0 + 0.3 * n(H)) * u[:, 0]).astype(np.float32)
    d["w3"] = (1.6 * n((H, N)) / H ** 0.5 / u).astype(np.float32)
    d["w4_words"], d["w4_scales"] = pack_weight(n((H, N)) / H ** 0.5 / u, "e4m3")
    return d

def reference(tab_words, tab_scales, offs, offs2, offs3, w1, w2_words, w2_scales, page0, wgs, ref, w3, w4_words, w4_scales):
    v = unpack_weight(tab_words, tab_scales, "e4m3")[:, unstriped(offs)]
    a = np.abs(mxq(f64(w1), 0, "e4m3").T @ v)
    b = unpack_weight(w2_words, w2_scales, "e2m1").T @ v
    h = np.abs(b - a)
    page = f64(page0).copy()
    page[:, unstriped(offs2)] = np.tile(f64(wgs), (H // 128, 1)) * h
    x = page[:, unstriped(offs3)] - f64(ref)[:, None]
    xq = mxq(x, 0, "e4m3")
    e = mxq(f64(w3), 0, "e4m3").T @ xq
    f = unpack_weight(w4_words, w4_scales, "e4m3").T @ xq
    gel = 0.5 * e * (1.0 + np.tanh((2.0 / np.pi) ** 0.5 * (e + 0.044715 * e ** 3)))
    y = gel + f
    words, scales = planes(page)
    return y, page, words, scales

@@ -1,0 +1,349 @@
+from contextlib import ExitStack
+
+import concourse.mybir as mybir
+from concourse.masks import make_identity
+
+F32 = mybir.dt.float32
+BF16 = mybir.dt.bfloat16
+I32 = mybir.dt.int32
+U32 = mybir.dt.uint32
+U16 = mybir.dt.uint16
+U8 = mybir.dt.uint8
+FP8X4 = mybir.dt.float8_e4m3fn_x4
+FP4X4 = mybir.dt.float4_e2m1fn_x4
+ACT = mybir.ActivationFunctionType
+ALU = mybir.AluOpType
+
+FLOPS = 4563402752
+
+P = 128
+PACK = 4
+PASSES = 3
+H = 512
+N = 640
+T = 4096
+S = 1024
+T2 = 2048
+HALF = 512
+QUADS = 4
+A_BANKS = 6
+PAGE_CHUNKS = 4
+SHIFT_ROWS = 112
+SCALAR_WEAVES = (0, 2)
+
+
+def tile_list_flue_liner_page_kernel(
+    tc, tab_words, tab_scales, offs, offs2, offs3, w1, w2_words, w2_scales, page0, wgs, ref, w3, w4_words, w4_scales,
+    out_0, out_1, out_2, out_3,
+):
+    nc = tc.nc
+    with ExitStack() as ctx:
+        lists = ctx.enter_context(tc.tile_pool(name="lists", bufs=1))
+        sb = ctx.enter_context(tc.tile_pool(name="sb", bufs=1))
+        psum = ctx.enter_context(tc.psum_pool(name="psum", bufs=1))
+
+        def bank(i, name):
+            return psum.tile([P, HALF], F32, tag="bank%d" % i, name=name)
+
+        list1 = lists.tile([P, S // 16], U16, name="list1")
+        list2 = lists.tile([P, S // 16], U16, name="list2")
+        list3 = lists.tile([P, S // 16], U16, name="list3")
+
+        tab = [sb.tile([P, T], U32, name="tab%d" % a, align_bytes=64) for a in range(PASSES)]
+        tab_sc = sb.tile([P, T], U8, name="tab_sc", align_bytes=64)
+        w2_w = sb.tile([P, PASSES, 2 * H], U8, name="w2_w", align_bytes=64)
+        w2_s = sb.tile([P, PASSES, H], U8, name="w2_s", align_bytes=64)
+        w4_w = sb.tile([P, N], U32, name="w4_w", align_bytes=64)
+        w4_s = sb.tile([P, N], U8, name="w4_s", align_bytes=64)
+        v_sc = sb.tile([P, S], U8, name="v_sc", align_bytes=64)
+        v_sc0 = [v_sc] + [sb.tile([P, S], U8, name="v_sc%d" % a, align_bytes=64) for a in range(1, PASSES)]
+        w1_raw = [sb.tile([P, PACK, H], F32, tag="raw%d" % a, name="w1_raw%d" % a, align_bytes=64) for a in range(PASSES)]
+        w3_raw = sb.tile([P, PACK, N], F32, name="w3_raw")
+        page = [sb.tile([P, T2], F32, name="page%d" % t) for t in range(PACK)]
+        gain = [sb.tile([P, S], F32, tag="gain", bufs=PACK, name="gain%d" % t) for t in range(PACK)]
+        ref_sb = sb.tile([P, PACK], F32, name="ref_sb")
+        neg_ref = sb.tile([P, PACK], F32, name="neg_ref")
+        ident = sb.tile([P, P], F32, name="ident")
+
+        nc.vector.memset(tab_sc[:].bitcast(I32), 0)
+        nc.vector.memset(w2_s[:].rearrange("p a c -> p (a c)").bitcast(I32), 0)
+        for a in range(1, PASSES):
+            nc.vector.memset(v_sc0[a][:].bitcast(I32), 0)
+        nc.vector.memset(w4_s[:].bitcast(I32), 0)
+
+        def load_tab(a, cols=slice(0, T)):
+            words = tab_words[a].rearrange("p t i -> p (t i)").bitcast(I32)
+            nc.sync.dma_start(out=tab[a][:, cols].bitcast(I32), in_=words[:, cols])
+
+        page_in = page0.rearrange("(p t) m -> t p m", t=PACK)
+        page_out = out_1.rearrange("(p t) m -> t p m", t=PACK)
+        gain_in = wgs.rearrange("(q t) j -> t q j", t=PACK)
+
+        def load_gain(t, cols=slice(0, S)):
+            for u in (0, 2, 1, 3):
+                nc.sync.dma_start(out=gain[t][32 * u : 32 * u + 32, cols], in_=gain_in[t][:, cols])
+
+        nc.sync.dma_start(list1[:], offs)
+        nc.sync.dma_start(list2[:], offs2)
+        nc.sync.dma_start(list3[:], offs3)
+        nc.sync.dma_start(out=ref_sb[:], in_=ref.rearrange("(p t) -> p t", t=PACK))
+        load_tab(0, slice(0, T // 2))
+        load_tab(0, slice(T // 2, T))
+        w2_in = w2_words.rearrange("a p b -> p a b").bitcast(I32)
+        nc.sync.dma_start(out=w2_w[:, 0:1].bitcast(I32), in_=w2_in[:, 0:1])
+        nc.sync.dma_start(out=w2_w[:, 1:PASSES].bitcast(I32), in_=w2_in[:, 1:PASSES])
+        for q in range(QUADS):
+            nc.sync.dma_start(
+                out=tab_sc[32 * q : 32 * q + 4 * PASSES, :].bitcast(I32),
+                in_=tab_scales[:, 4 * q : 4 * q + 4, :].bitcast(I32),
+            )
+        load_tab(1)
+        for q in range(QUADS):
+            nc.sync.dma_start(
+                out=w2_s[32 * q : 32 * q + 4].bitcast(I32),
+                in_=w2_scales[:, 4 * q : 4 * q + 4, :].rearrange("a r c -> r a c").bitcast(I32),
+            )
+        load_tab(2)
+        for a in range(PASSES):
+            nc.sync.dma_start(out=w1_raw[a][:], in_=w1[H * a : H * (a + 1), :].rearrange("(p j) c -> p j c", j=PACK))
+        load_gain(0, slice(0, HALF))
+        nc.sync.dma_start(out=page[0][:], in_=page_in[0])
+        load_gain(0, slice(HALF, S))
+        nc.sync.dma_start(out=page[1][:], in_=page_in[1])
+        load_gain(1)
+        nc.sync.dma_start(out=w3_raw[:], in_=w3.rearrange("(p j) n -> p j n", j=PACK))
+        nc.sync.dma_start(out=page[2][:], in_=page_in[2])
+        load_gain(2)
+        nc.sync.dma_start(out=page[3][:], in_=page_in[3])
+        load_gain(3)
+        nc.sync.dma_start(out=w4_w[:].bitcast(I32), in_=w4_words[0].rearrange("p c i -> p (c i)").bitcast(I32))
+        for q in range(QUADS):
+            nc.sync.dma_start(
+                out=w4_s[32 * q : 32 * q + 4, :].bitcast(I32), in_=w4_scales[0, 4 * q : 4 * q + 4, :].bitcast(I32)
+            )
+
+        nc.vector.tensor_copy(out=v_sc[:], in_=tab_sc[:].indirect(list1[:]))
+        for a in range(1, PASSES):
+            nc.scalar.dma_start(out=v_sc0[a][0:SHIFT_ROWS, :].bitcast(I32), in_=v_sc[4 * a : 4 * a + SHIFT_ROWS, :].bitcast(I32))
+        make_identity(nc, ident[:])
+        v_w = [sb.tile([P, S], U32, name="v_w%d" % a, align_bytes=64) for a in range(PASSES)]
+        blocks = S // P
+        b_bank = [bank(jb, "b_bank%d" % jb) for jb in range(blocks)]
+        neg_b = sb.tile([P, blocks * H], F32, tag="big", name="neg_b", align_bytes=64)
+        for a in range(PASSES):
+            if a < PASSES - 1:
+                nc.vector.tensor_copy(out=v_w[a][:], in_=tab[a][:].indirect(list1[:]))
+            else:
+                for h in range(2):
+                    nc.vector.tensor_copy(
+                        out=v_w[a][:, HALF * h : HALF * (h + 1)],
+                        in_=tab[a][:].indirect(list1[:, 32 * h : 32 * (h + 1)]),
+                    )
+            for jb in range(blocks):
+                cols = slice(P * jb, P * (jb + 1))
+                nc.tensor.matmul_mx(
+                    out=b_bank[jb][:],
+                    lhsT=v_w[a][:, cols].bitcast(FP8X4),
+                    lhsT_scale=v_sc0[a][:, cols],
+                    rhs=w2_w[:, a, :].bitcast(FP4X4),
+                    rhs_scale=w2_s[:, a, :],
+                    start=(a == 0),
+                    stop=(a == PASSES - 1),
+                )
+                if a == PASSES - 1:
+                    nc.scalar.activation(
+                        out=neg_b[:, H * jb : H * (jb + 1)].rearrange("j (t p) -> j t p", t=PACK),
+                        in_=b_bank[jb][:].rearrange("j (p t) -> j t p", t=PACK),
+                        func=ACT.Copy,
+                        scale=-1.0,
+                    )
+        nc.scalar.mul(neg_ref[:], ref_sb[:], -1.0)
+
+        w1_q = [sb.tile([P, H], U32, name="w1_q%d" % a, align_bytes=64) for a in range(PASSES)]
+        w1_s = [sb.tile([P, H], U8, name="w1_s%d" % a, align_bytes=64) for a in range(PASSES)]
+        w1_b = []
+        for a in range(PASSES):
+            w1_b.append(sb.tile([P, PACK * H], BF16, tag="stage", bufs=2, name="w1_b%d" % a, align_bytes=64))
+            if a < PASSES - 1:
+                nc.vector.tensor_copy(
+                    out=w1_b[a][:].rearrange("p (t m j) -> p m j t", t=PACK, j=PACK),
+                    in_=w1_raw[a][:].rearrange("p j (m t) -> p m j t", t=PACK),
+                )
+                nc.vector.quantize_mx(out=w1_q[a][:].bitcast(FP8X4), scales=w1_s[a][:], in_=w1_b[a][:])
+        last = PASSES - 1
+        last_by_t = w1_raw[last][:].rearrange("p j (m t) -> p t m j", t=PACK)
+        for t in range(PACK + 1):
+            if t < PACK:
+                nc.vector.tensor_copy(
+                    out=w1_b[last][:, H * t : H * (t + 1)].rearrange("p (m j) -> p m j", j=PACK), in_=last_by_t[:, t]
+                )
+            if t > 0:
+                cols = slice(P * (t - 1), P * t)
+                nc.vector.quantize_mx(
+                    out=w1_q[last][:, cols].bitcast(FP8X4),
+                    scales=w1_s[last][:, cols],
+                    in_=w1_b[last][:, H * (t - 1) : H * t],
+                )
+
+        groups = 2 * PACK
+        a_bank = {}
+
+        def a_pass(g, a):
+            t, h = divmod(g, 2)
+            if a == 0:
+                a_bank[g] = bank(g % A_BANKS, "a_bank%d" % g)
+            for i in range(4):
+                cols = slice(HALF * h + P * i, HALF * h + P * (i + 1))
+                nc.tensor.matmul_mx(
+                    out=a_bank[g][:, P * i : P * (i + 1)],
+                    lhsT=v_w[a][:, cols].bitcast(FP8X4),
+                    lhsT_scale=v_sc0[a][:, cols],
+                    rhs=w1_q[a][:, P * t : P * (t + 1)].bitcast(FP8X4),
+                    rhs_scale=w1_s[a][:, P * t : P * (t + 1)],
+                    start=(a == 0 and i == 0),
+                    stop=(a == last and i == 3),
+                )
+
+        for a in range(last):
+            for g in range(A_BANKS):
+                a_pass(g, a)
+        dev = []
+        for g in range(groups):
+            t, h = divmod(g, 2)
+            if g >= A_BANKS:
+                for a in range(last):
+                    a_pass(g, a)
+            a_pass(g, last)
+            abs_a = sb.tile([P, HALF], F32, tag="small", bufs=3, name="abs_a%d" % g)
+            nc.scalar.activation(out=abs_a[:], in_=a_bank[g][:], func=ACT.Abs)
+            d_bank = bank(A_BANKS + g % 2, "d_bank%d" % g)
+            for i in range(4):
+                jb = 4 * h + i
+                out_cols = d_bank[:, P * i : P * (i + 1)]
+                nc.tensor.matmul(
+                    out_cols, lhsT=neg_b[:, H * jb + P * t : H * jb + P * (t + 1)], rhs=ident[:],
+                    is_transpose=True, start=True, stop=False,
+                )
+                nc.tensor.matmul(
+                    out_cols, lhsT=abs_a[:, P * i : P * (i + 1)], rhs=ident[:], is_transpose=True, start=False, stop=True
+                )
+            if h == 0:
+                dev.append(sb.tile([P, S], F32, tag="mid", bufs=4, name="dev%d" % t))
+            nc.scalar.activation(out=dev[t][:, HALF * h : HALF * (h + 1)], in_=d_bank[:], func=ACT.Abs)
+
+        picked = sb.tile([P, 2 * S], F32, tag="raw0", name="picked", align_bytes=64)
+        x_b = sb.tile([P, PACK * S], BF16, tag="raw1", name="x_b", align_bytes=64)
+        rounded = sb.tile([P, PACK * (T2 + S + N)], BF16, tag="big", name="rounded", align_bytes=64)
+        p_pairs = rounded[:, 0 : PACK * T2]
+        x_pairs = rounded[:, PACK * T2 : PACK * (T2 + S)]
+        w3_b = rounded[:, PACK * (T2 + S) :]
+        x_view = x_pairs.rearrange("p (c u j e) -> p u e c j", c=2, u=2, e=2)
+        p_view = p_pairs.rearrange("p (c u m e) -> p u e c m", c=PAGE_CHUNKS, u=2, e=2)
+
+        def scatter(t):
+            if t == 0:
+                for h in range(2):
+                    cols = slice(HALF * h, HALF * (h + 1))
+                    nc.vector.tensor_tensor(
+                        out=page[t][:].indirect(list2[:, 32 * h : 32 * (h + 1)]),
+                        in0=dev[t][:, cols], in1=gain[t][:, cols], op=ALU.mult,
+                    )
+            else:
+                nc.vector.tensor_tensor(out=page[t][:].indirect(list2[:]), in0=dev[t][:], in1=gain[t][:], op=ALU.mult)
+            nc.sync.dma_start(out=page_out[t], in_=page[t][:])
+
+        def fetch(t):
+            slot = picked[:, S * (t % 2) : S * (t % 2 + 1)]
+            nc.vector.tensor_copy(out=slot, in_=page[t][:].indirect(list3[:]))
+            nc.scalar.activation(
+                out=x_view[:, t // 2, t % 2], in_=slot.rearrange("p (c j) -> p c j", c=2),
+                func=ACT.Identity, bias=neg_ref[:, t : t + 1],
+            )
+            nc.scalar.copy(
+                out=p_view[:, t // 2, t % 2], in_=page[t][:].rearrange("p (c m) -> p c m", c=PAGE_CHUNKS)
+            )
+
+        w3_q = sb.tile([P, N], U32, name="w3_q", align_bytes=64)
+        w3_s = sb.tile([P, N], U8, name="w3_s", align_bytes=64)
+
+        scatter(0)
+        scatter(1)
+        fetch(0)
+        nc.scalar.copy(
+            out=w3_b.rearrange("p (c i j) -> p c j i", i=4, j=PACK),
+            in_=w3_raw[:].rearrange("p j (c i) -> p c j i", i=4),
+        )
+        scatter(2)
+        fetch(1)
+        for lo, hi in ((0, HALF), (HALF, N)):
+            nc.vector.quantize_mx(
+                out=w3_q[:, lo:hi].bitcast(FP8X4), scales=w3_s[:, lo:hi], in_=w3_b[:, PACK * lo : PACK * hi]
+            )
+        fetch(2)
+        scatter(3)
+
+        t = PACK - 1
+        x_q = sb.tile([P, S], U32, name="x_q", align_bytes=64)
+        x_s = sb.tile([P, S], U8, name="x_s", align_bytes=64)
+        for h in range(2):
+            slot = picked[:, S + HALF * h : S + HALF * (h + 1)]
+            nc.vector.tensor_copy(out=slot, in_=page[t][:].indirect(list3[:, 32 * h : 32 * (h + 1)]))
+            nc.scalar.activation(out=x_view[:, 1, 1, h], in_=slot, func=ACT.Identity, bias=neg_ref[:, t : t + 1])
+        for h in range(2):
+            span = slice(PACK * HALF * h, PACK * HALF * (h + 1))
+            cols = slice(HALF * h, HALF * (h + 1))
+            nc.vector.tensor_copy(
+                out=x_b[:, span].bitcast(I32).rearrange("p (j u) -> p j u", u=2),
+                in_=x_pairs[:, span].bitcast(I32).rearrange("p (u j) -> p j u", u=2),
+            )
+            nc.vector.quantize_mx(out=x_q[:, cols].bitcast(FP8X4), scales=x_s[:, cols], in_=x_b[:, span])
+
+        p_q = sb.tile([P, T2], U32, tag="raw2", name="p_q", align_bytes=64)
+        p_s = sb.tile([P, T2], U8, name="p_s", align_bytes=64)
+        words_out = out_2[0].rearrange("p m t -> p (m t)").bitcast(I32)
+
+        def planes(c):
+            cols = slice(HALF * c, HALF * (c + 1))
+            span = slice(PACK * HALF * c, PACK * HALF * (c + 1))
+            nc.scalar.copy(out=p_view[:, 1, 1, c], in_=page[t][:, cols])
+            p_b = sb.tile([P, PACK * HALF], BF16, tag="stage", bufs=2, name="p_b%d" % c, align_bytes=64)
+            if c in SCALAR_WEAVES:
+                nc.scalar.copy(
+                    out=p_b[:].bitcast(U32).rearrange("p (m u) -> p m u", u=2),
+                    in_=p_pairs[:, span].bitcast(U32).rearrange("p (u m) -> p m u", u=2),
+                )
+            else:
+                nc.vector.tensor_copy(
+                    out=p_b[:].bitcast(I32).rearrange("p (m u) -> p m u", u=2),
+                    in_=p_pairs[:, span].bitcast(I32).rearrange("p (u m) -> p m u", u=2),
+                )
+            nc.vector.quantize_mx(out=p_q[:, cols].bitcast(FP8X4), scales=p_s[:, cols], in_=p_b[:])
+            nc.sync.dma_start(out=words_out[:, cols], in_=p_q[:, cols].bitcast(I32))
+
+        def second_stage(i):
+            h, nt = divmod(i, N // P)
+            cols = slice(HALF * h, HALF * (h + 1))
+            rows = slice(P * nt, P * (nt + 1))
+            e_bank = bank((2 * i) % 8, "e_bank%d" % i)
+            f_bank = bank((2 * i + 1) % 8, "f_bank%d" % i)
+            for acc, words, scales in ((e_bank, w3_q, w3_s), (f_bank, w4_w, w4_s)):
+                nc.tensor.matmul_mx(
+                    out=acc[:], lhsT=words[:, rows].bitcast(FP8X4), lhsT_scale=scales[:, rows],
+                    rhs=x_q[:, cols].bitcast(FP8X4), rhs_scale=x_s[:, cols], start=True, stop=True,
+                )
+            gel = sb.tile([P, HALF], F32, tag="small", bufs=3, name="gel%d" % i)
+            nc.scalar.activation(out=gel[:], in_=e_bank[:], func=ACT.Gelu_apprx_tanh)
+            y = sb.tile([P, HALF], F32, tag=("mid", "gain")[i % 2], bufs=4, name="y%d" % i)
+            nc.vector.tensor_tensor(out=y[:], in0=f_bank[:], in1=gel[:], op=ALU.add)
+            nc.sync.dma_start(out=out_0[rows, cols], in_=y[:])
+
+        planes(0)
+        for i in range(2 * (N // P)):
+            second_stage(i)
+            if i in (1, 3, 5):
+                planes((i + 1) // 2)
+            if i == 5:
+                for q in range(QUADS):
+                    nc.sync.dma_start(
+                        out=out_3[0, 4 * q : 4 * q + 4, :].bitcast(I32), in_=p_s[32 * q : 32 * q + 4, :].bitcast(I32)
+                    )

@@ -26,10 +26,12 @@ S = 1024
 T2 = 2048
 HALF = 512
 QUADS = 4
-A_BANKS = 6
+A_BANKS = (0, 2, 3, 4, 6, 7)
+D_BANKS = (1, 5)
 PAGE_CHUNKS = 4
-SHIFT_ROWS = 112
-SCALAR_WEAVES = (0, 2)
+VECTOR_TURNS = ((1, 1), (3, 1))
+LATE_BANKS = (0, 1, 2, 5)
+HELD_BANKS = (3, 4, 6, 7)
 
 
 def tile_list_flue_liner_page_kernel(
@@ -56,133 +58,133 @@ def tile_list_flue_liner_page_kernel(
         w4_w = sb.tile([P, N], U32, name="w4_w", align_bytes=64)
         w4_s = sb.tile([P, N], U8, name="w4_s", align_bytes=64)
         v_sc = sb.tile([P, S], U8, name="v_sc", align_bytes=64)
-        v_sc0 = [v_sc] + [sb.tile([P, S], U8, name="v_sc%d" % a, align_bytes=64) for a in range(1, PASSES)]
+        v_planes = sb.tile([P, PASSES, S], U8, name="v_planes", align_bytes=64)
         w1_raw = [sb.tile([P, PACK, H], F32, tag="raw%d" % a, name="w1_raw%d" % a, align_bytes=64) for a in range(PASSES)]
-        w3_raw = sb.tile([P, PACK, N], F32, name="w3_raw")
+        w3_raw = sb.tile([P, PACK, N], F32, tag="raw3", name="w3_raw", align_bytes=64)
         page = [sb.tile([P, T2], F32, name="page%d" % t) for t in range(PACK)]
-        gain = [sb.tile([P, S], F32, tag="gain", bufs=PACK, name="gain%d" % t) for t in range(PACK)]
-        ref_sb = sb.tile([P, PACK], F32, name="ref_sb")
+        gain = sb.tile([P, S], F32, name="gain")
+        ref_rows = sb.tile([P, P], F32, name="ref_rows")
         neg_ref = sb.tile([P, PACK], F32, name="neg_ref")
         ident = sb.tile([P, P], F32, name="ident")
 
         nc.vector.memset(tab_sc[:].bitcast(I32), 0)
         nc.vector.memset(w2_s[:].rearrange("p a c -> p (a c)").bitcast(I32), 0)
-        for a in range(1, PASSES):
-            nc.vector.memset(v_sc0[a][:].bitcast(I32), 0)
+        nc.vector.memset(v_planes[:].rearrange("p a j -> p (a j)").bitcast(I32), 0)
         nc.vector.memset(w4_s[:].bitcast(I32), 0)
+        nc.gpsimd.memset(ref_rows[:], 0.0)
 
         def load_tab(a, cols=slice(0, T)):
             words = tab_words[a].rearrange("p t i -> p (t i)").bitcast(I32)
             nc.sync.dma_start(out=tab[a][:, cols].bitcast(I32), in_=words[:, cols])
 
-        page_in = page0.rearrange("(p t) m -> t p m", t=PACK)
-        page_out = out_1.rearrange("(p t) m -> t p m", t=PACK)
-        gain_in = wgs.rearrange("(q t) j -> t q j", t=PACK)
+        def load_w4_scales(lo, hi):
+            for q in range(lo, hi):
+                nc.sync.dma_start(
+                    out=w4_s[32 * q : 32 * q + 4, :].bitcast(I32), in_=w4_scales[0, 4 * q : 4 * q + 4, :].bitcast(I32)
+                )
 
-        def load_gain(t, cols=slice(0, S)):
-            for u in (0, 2, 1, 3):
-                nc.sync.dma_start(out=gain[t][32 * u : 32 * u + 32, cols], in_=gain_in[t][:, cols])
+        page_in = page0.rearrange("(t p) m -> t p m", p=P)
+        page_out = out_1.rearrange("(t p) m -> t p m", p=P)
 
         nc.sync.dma_start(list1[:], offs)
         nc.sync.dma_start(list2[:], offs2)
         nc.sync.dma_start(list3[:], offs3)
-        nc.sync.dma_start(out=ref_sb[:], in_=ref.rearrange("(p t) -> p t", t=PACK))
         load_tab(0, slice(0, T // 2))
         load_tab(0, slice(T // 2, T))
         w2_in = w2_words.rearrange("a p b -> p a b").bitcast(I32)
-        nc.sync.dma_start(out=w2_w[:, 0:1].bitcast(I32), in_=w2_in[:, 0:1])
-        nc.sync.dma_start(out=w2_w[:, 1:PASSES].bitcast(I32), in_=w2_in[:, 1:PASSES])
-        for q in range(QUADS):
-            nc.sync.dma_start(
-                out=tab_sc[32 * q : 32 * q + 4 * PASSES, :].bitcast(I32),
-                in_=tab_scales[:, 4 * q : 4 * q + 4, :].bitcast(I32),
-            )
-        load_tab(1)
+        for a in range(PASSES):
+            nc.sync.dma_start(out=w2_w[:, a].bitcast(I32), in_=w2_in[:, a])
+        nc.sync.dma_start(
+            out=tab_sc[0 : 16 * PASSES, :].bitcast(I32), in_=tab_scales.rearrange("a q t -> q a t").bitcast(I32)
+        )
+        load_tab(1, slice(0, T // 2))
+        load_tab(1, slice(T // 2, 3 * T // 4))
+        load_tab(1, slice(3 * T // 4, T))
         for q in range(QUADS):
             nc.sync.dma_start(
                 out=w2_s[32 * q : 32 * q + 4].bitcast(I32),
                 in_=w2_scales[:, 4 * q : 4 * q + 4, :].rearrange("a r c -> r a c").bitcast(I32),
             )
+        nc.sync.dma_start(out=ref_rows[0:PACK, :], in_=ref.rearrange("(t p) -> t p", p=P))
         load_tab(2)
-        for a in range(PASSES):
-            nc.sync.dma_start(out=w1_raw[a][:], in_=w1[H * a : H * (a + 1), :].rearrange("(p j) c -> p j c", j=PACK))
-        load_gain(0, slice(0, HALF))
-        nc.sync.dma_start(out=page[0][:], in_=page_in[0])
-        load_gain(0, slice(HALF, S))
-        nc.sync.dma_start(out=page[1][:], in_=page_in[1])
-        load_gain(1)
-        nc.sync.dma_start(out=w3_raw[:], in_=w3.rearrange("(p j) n -> p j n", j=PACK))
-        nc.sync.dma_start(out=page[2][:], in_=page_in[2])
-        load_gain(2)
-        nc.sync.dma_start(out=page[3][:], in_=page_in[3])
-        load_gain(3)
-        nc.sync.dma_start(out=w4_w[:].bitcast(I32), in_=w4_words[0].rearrange("p c i -> p (c i)").bitcast(I32))
+        nc.vector.tensor_copy(out=v_sc[:], in_=tab_sc[:].indirect(list1[:]))
         for q in range(QUADS):
             nc.sync.dma_start(
-                out=w4_s[32 * q : 32 * q + 4, :].bitcast(I32), in_=w4_scales[0, 4 * q : 4 * q + 4, :].bitcast(I32)
+                out=v_planes[32 * q : 32 * q + 4].bitcast(I32),
+                in_=v_sc[4 * PASSES * q : 4 * PASSES * (q + 1), :].bitcast(I32),
             )
+        for a in range(PASSES):
+            nc.sync.dma_start(out=w1_raw[a][:], in_=w1[H * a : H * (a + 1), :].rearrange("(p j) c -> p j c", j=PACK))
+        nc.sync.dma_start(out=gain[:, 0:HALF], in_=wgs[:, 0:HALF])
+        nc.sync.dma_start(out=page[0][:], in_=page_in[0])
+        nc.sync.dma_start(out=gain[:, HALF:S], in_=wgs[:, HALF:S])
+        nc.sync.dma_start(out=page[1][:], in_=page_in[1])
+        nc.sync.dma_start(out=w3_raw[:], in_=w3.rearrange("(p j) n -> p j n", j=PACK))
+        nc.sync.dma_start(out=page[2][:], in_=page_in[2])
+        nc.sync.dma_start(out=page[3][:], in_=page_in[3])
+        nc.sync.dma_start(out=w4_w[:].bitcast(I32), in_=w4_words[0].rearrange("p c i -> p (c i)").bitcast(I32))
+        load_w4_scales(0, QUADS)
 
-        nc.vector.tensor_copy(out=v_sc[:], in_=tab_sc[:].indirect(list1[:]))
-        for a in range(1, PASSES):
-            nc.scalar.dma_start(out=v_sc0[a][0:SHIFT_ROWS, :].bitcast(I32), in_=v_sc[4 * a : 4 * a + SHIFT_ROWS, :].bitcast(I32))
         make_identity(nc, ident[:])
+        ref_bank = bank(7, "ref_bank")
+        nc.tensor.transpose(ref_bank[:, 0:P], ref_rows[:], ident[:])
+        nc.scalar.activation(out=neg_ref[:], in_=ref_bank[:, 0:PACK], func=ACT.Copy, scale=-1.0)
         v_w = [sb.tile([P, S], U32, name="v_w%d" % a, align_bytes=64) for a in range(PASSES)]
         blocks = S // P
         b_bank = [bank(jb, "b_bank%d" % jb) for jb in range(blocks)]
         neg_b = sb.tile([P, blocks * H], F32, tag="big", name="neg_b", align_bytes=64)
         for a in range(PASSES):
-            if a < PASSES - 1:
-                nc.vector.tensor_copy(out=v_w[a][:], in_=tab[a][:].indirect(list1[:]))
-            else:
-                for h in range(2):
-                    nc.vector.tensor_copy(
-                        out=v_w[a][:, HALF * h : HALF * (h + 1)],
-                        in_=tab[a][:].indirect(list1[:, 32 * h : 32 * (h + 1)]),
-                    )
-            for jb in range(blocks):
-                cols = slice(P * jb, P * (jb + 1))
-                nc.tensor.matmul_mx(
-                    out=b_bank[jb][:],
-                    lhsT=v_w[a][:, cols].bitcast(FP8X4),
-                    lhsT_scale=v_sc0[a][:, cols],
-                    rhs=w2_w[:, a, :].bitcast(FP4X4),
-                    rhs_scale=w2_s[:, a, :],
-                    start=(a == 0),
-                    stop=(a == PASSES - 1),
+            pieces = 2 if a == PASSES - 1 else 1
+            for h in range(pieces):
+                n = S // pieces
+                nc.vector.tensor_copy(
+                    out=v_w[a][:, n * h : n * (h + 1)], in_=tab[a][:].indirect(list1[:, n // 16 * h : n // 16 * (h + 1)])
                 )
-                if a == PASSES - 1:
-                    nc.scalar.activation(
-                        out=neg_b[:, H * jb : H * (jb + 1)].rearrange("j (t p) -> j t p", t=PACK),
-                        in_=b_bank[jb][:].rearrange("j (p t) -> j t p", t=PACK),
-                        func=ACT.Copy,
-                        scale=-1.0,
-                    )
-        nc.scalar.mul(neg_ref[:], ref_sb[:], -1.0)
+
+        def b_pass(jb, a):
+            cols = slice(P * jb, P * (jb + 1))
+            nc.tensor.matmul_mx(
+                out=b_bank[jb][:],
+                lhsT=v_w[a][:, cols].bitcast(FP8X4),
+                lhsT_scale=v_planes[:, a, cols],
+                rhs=w2_w[:, a, :].bitcast(FP4X4),
+                rhs_scale=w2_s[:, a, :],
+                start=(a == 0),
+                stop=(a == PASSES - 1),
+            )
+
+        for jb in range(blocks):
+            for a in range(PASSES):
+                b_pass(jb, a)
+
+        def negate_b(h):
+            for jb in range(4 * h, 4 * h + 4):
+                nc.scalar.activation(out=neg_b[:, H * jb : H * (jb + 1)], in_=b_bank[jb][:], func=ACT.Copy, scale=-1.0)
+
+        negate_b(0)
 
         w1_q = [sb.tile([P, H], U32, name="w1_q%d" % a, align_bytes=64) for a in range(PASSES)]
         w1_s = [sb.tile([P, H], U8, name="w1_s%d" % a, align_bytes=64) for a in range(PASSES)]
-        w1_b = []
-        for a in range(PASSES):
-            w1_b.append(sb.tile([P, PACK * H], BF16, tag="stage", bufs=2, name="w1_b%d" % a, align_bytes=64))
-            if a < PASSES - 1:
-                nc.vector.tensor_copy(
-                    out=w1_b[a][:].rearrange("p (t m j) -> p m j t", t=PACK, j=PACK),
-                    in_=w1_raw[a][:].rearrange("p j (m t) -> p m j t", t=PACK),
-                )
-                nc.vector.quantize_mx(out=w1_q[a][:].bitcast(FP8X4), scales=w1_s[a][:], in_=w1_b[a][:])
         last = PASSES - 1
-        last_by_t = w1_raw[last][:].rearrange("p j (m t) -> p t m j", t=PACK)
-        for t in range(PACK + 1):
-            if t < PACK:
+
+        for a in range(PASSES):
+            staged = sb.tile([P, PACK * H], BF16, tag="stage", bufs=2, name="w1_b%d" % a, align_bytes=64)
+            width = P if a == last else H
+            for lo in range(0, H, width):
+                rounded_cols = staged[:, PACK * lo : PACK * (lo + width)]
                 nc.vector.tensor_copy(
-                    out=w1_b[last][:, H * t : H * (t + 1)].rearrange("p (m j) -> p m j", j=PACK), in_=last_by_t[:, t]
+                    out=rounded_cols.rearrange("p (c i j) -> p c j i", i=4, j=PACK),
+                    in_=w1_raw[a][:, :, lo : lo + width].rearrange("p j (c i) -> p c j i", i=4),
                 )
-            if t > 0:
-                cols = slice(P * (t - 1), P * t)
                 nc.vector.quantize_mx(
-                    out=w1_q[last][:, cols].bitcast(FP8X4),
-                    scales=w1_s[last][:, cols],
-                    in_=w1_b[last][:, H * (t - 1) : H * t],
+                    out=w1_q[a][:, lo : lo + width].bitcast(FP8X4), scales=w1_s[a][:, lo : lo + width], in_=rounded_cols
+                )
+
+        def add_turned(acc, parts, opens):
+            for i, block in enumerate(parts):
+                nc.tensor.matmul(
+                    acc[:, P * i : P * (i + 1)], lhsT=block, rhs=ident[:], is_transpose=True,
+                    start=(opens and i == 0), stop=(not opens and i == 3),
                 )
 
         groups = 2 * PACK
@@ -191,54 +193,49 @@ def tile_list_flue_liner_page_kernel(
         def a_pass(g, a):
             t, h = divmod(g, 2)
             if a == 0:
-                a_bank[g] = bank(g % A_BANKS, "a_bank%d" % g)
+                a_bank[g] = bank(A_BANKS[g % len(A_BANKS)], "a_bank%d" % g)
             for i in range(4):
                 cols = slice(HALF * h + P * i, HALF * h + P * (i + 1))
                 nc.tensor.matmul_mx(
                     out=a_bank[g][:, P * i : P * (i + 1)],
                     lhsT=v_w[a][:, cols].bitcast(FP8X4),
-                    lhsT_scale=v_sc0[a][:, cols],
+                    lhsT_scale=v_planes[:, a, cols],
                     rhs=w1_q[a][:, P * t : P * (t + 1)].bitcast(FP8X4),
                     rhs_scale=w1_s[a][:, P * t : P * (t + 1)],
                     start=(a == 0 and i == 0),
                     stop=(a == last and i == 3),
                 )
 
-        for a in range(last):
-            for g in range(A_BANKS):
-                a_pass(g, a)
         dev = []
         for g in range(groups):
             t, h = divmod(g, 2)
-            if g >= A_BANKS:
-                for a in range(last):
-                    a_pass(g, a)
-            a_pass(g, last)
-            abs_a = sb.tile([P, HALF], F32, tag="small", bufs=3, name="abs_a%d" % g)
+            if g == 1:
+                negate_b(1)
+            for a in range(PASSES):
+                a_pass(g, a)
+            abs_a = sb.tile([P, HALF], F32, tag="abs", bufs=3, name="abs_a%d" % g)
             nc.scalar.activation(out=abs_a[:], in_=a_bank[g][:], func=ACT.Abs)
-            d_bank = bank(A_BANKS + g % 2, "d_bank%d" % g)
-            for i in range(4):
-                jb = 4 * h + i
-                out_cols = d_bank[:, P * i : P * (i + 1)]
-                nc.tensor.matmul(
-                    out_cols, lhsT=neg_b[:, H * jb + P * t : H * jb + P * (t + 1)], rhs=ident[:],
-                    is_transpose=True, start=True, stop=False,
-                )
-                nc.tensor.matmul(
-                    out_cols, lhsT=abs_a[:, P * i : P * (i + 1)], rhs=ident[:], is_transpose=True, start=False, stop=True
-                )
+            d_bank = bank(D_BANKS[g % 2], "d_bank%d" % g)
+            first = [neg_b[:, H * (4 * h + i) + P * t : H * (4 * h + i) + P * (t + 1)] for i in range(4)]
+            add_turned(d_bank, first, True)
+            add_turned(d_bank, [abs_a[:, P * i : P * (i + 1)] for i in range(4)], False)
             if h == 0:
-                dev.append(sb.tile([P, S], F32, tag="mid", bufs=4, name="dev%d" % t))
+                tag, bufs = ("last", 1) if t == PACK - 1 else ("mid", 3)
+                dev.append(sb.tile([P, S], F32, tag=tag, bufs=bufs, name="dev%d" % t))
             nc.scalar.activation(out=dev[t][:, HALF * h : HALF * (h + 1)], in_=d_bank[:], func=ACT.Abs)
 
-        picked = sb.tile([P, 2 * S], F32, tag="raw0", name="picked", align_bytes=64)
-        x_b = sb.tile([P, PACK * S], BF16, tag="raw1", name="x_b", align_bytes=64)
+        picked = [sb.tile([P, S], F32, tag="raw%d" % n, name="picked%d" % n, align_bytes=64) for n in range(2)]
+        x_b = sb.tile([P, PACK * S], BF16, tag="raw2", name="x_b", align_bytes=64)
         rounded = sb.tile([P, PACK * (T2 + S + N)], BF16, tag="big", name="rounded", align_bytes=64)
-        p_pairs = rounded[:, 0 : PACK * T2]
-        x_pairs = rounded[:, PACK * T2 : PACK * (T2 + S)]
+        p_turned = rounded[:, 0 : PACK * T2]
+        x_turned = rounded[:, PACK * T2 : PACK * (T2 + S)]
         w3_b = rounded[:, PACK * (T2 + S) :]
-        x_view = x_pairs.rearrange("p (c u j e) -> p u e c j", c=2, u=2, e=2)
-        p_view = p_pairs.rearrange("p (c u m e) -> p u e c m", c=PAGE_CHUNKS, u=2, e=2)
+        ring = list(LATE_BANKS)
+
+        def next_bank(name):
+            n = ring.pop(0)
+            ring.append(n)
+            return bank(n, name)
 
         def scatter(t):
             if t == 0:
@@ -246,77 +243,108 @@ def tile_list_flue_liner_page_kernel(
                     cols = slice(HALF * h, HALF * (h + 1))
                     nc.vector.tensor_tensor(
                         out=page[t][:].indirect(list2[:, 32 * h : 32 * (h + 1)]),
-                        in0=dev[t][:, cols], in1=gain[t][:, cols], op=ALU.mult,
+                        in0=dev[t][:, cols], in1=gain[:, cols], op=ALU.mult,
                     )
             else:
-                nc.vector.tensor_tensor(out=page[t][:].indirect(list2[:]), in0=dev[t][:], in1=gain[t][:], op=ALU.mult)
+                nc.vector.tensor_tensor(out=page[t][:].indirect(list2[:]), in0=dev[t][:], in1=gain[:], op=ALU.mult)
             nc.sync.dma_start(out=page_out[t], in_=page[t][:])
 
-        def fetch(t):
-            slot = picked[:, S * (t % 2) : S * (t % 2 + 1)]
-            nc.vector.tensor_copy(out=slot, in_=page[t][:].indirect(list3[:]))
-            nc.scalar.activation(
-                out=x_view[:, t // 2, t % 2], in_=slot.rearrange("p (c j) -> p c j", c=2),
-                func=ACT.Identity, bias=neg_ref[:, t : t + 1],
-            )
+        def round_out(acc, turned, c, t):
+            view = turned[:, PACK * HALF * c : PACK * HALF * (c + 1)].rearrange("m (k u t w) -> m t k u w", k=4, u=2, t=PACK)
             nc.scalar.copy(
-                out=p_view[:, t // 2, t % 2], in_=page[t][:].rearrange("p (c m) -> p c m", c=PAGE_CHUNKS)
+                out=view[:, t].rearrange("m k u (q e) -> m k u q e", e=2),
+                in_=acc[:].rearrange("m (k q u e) -> m k u q e", k=4, u=2, e=2),
             )
+
+        def turn_page(t, c):
+            acc = next_bank("pt_bank%d_%d" % (t, c))
+            for i in range(4):
+                col = HALF * c + P * i
+                nc.tensor.transpose(acc[:, P * i : P * (i + 1)], page[t][:, col : col + P], ident[:])
+            round_out(acc, p_turned, c, t)
+
+        def open_x(acc, t):
+            add_turned(acc, [neg_ref[:, t : t + 1].to_broadcast([P, P])] * 4, True)
+
+        def close_x(acc, t, h):
+            col = HALF * h
+            add_turned(acc, [picked[t % 2][:, col + P * i : col + P * (i + 1)] for i in range(4)], False)
+            round_out(acc, x_turned, h, t)
+
+        def turn_back(turned, c, half, dst, on_vector, name):
+            acc = next_bank(name)
+            words = turned[:, PACK * HALF * c + 2 * HALF * half : PACK * HALF * c + 2 * HALF * (half + 1)].bitcast(F32)
+            for i in range(4):
+                nc.tensor.transpose(acc[:, P * i : P * (i + 1)], words[:, P * i : P * (i + 1)], ident[:])
+            out = dst[:, 2 * HALF * half : 2 * HALF * (half + 1)].bitcast(F32).rearrange("p (k m u) -> p k m u", k=2, u=2)
+            src = acc[:].rearrange("p (k u m) -> p k m u", k=2, u=2)
+            if on_vector:
+                nc.vector.tensor_copy(out=out, in_=src)
+            else:
+                nc.scalar.copy(out=out, in_=src)
+
+        def fetch(t):
+            nc.vector.tensor_copy(out=picked[t % 2][:], in_=page[t][:].indirect(list3[:]))
+            for c in range(PAGE_CHUNKS):
+                turn_page(t, c)
+            for h in range(2):
+                acc = next_bank("xt_bank%d_%d" % (t, h))
+                open_x(acc, t)
+                close_x(acc, t, h)
 
         w3_q = sb.tile([P, N], U32, name="w3_q", align_bytes=64)
         w3_s = sb.tile([P, N], U8, name="w3_s", align_bytes=64)
 
         scatter(0)
         scatter(1)
-        fetch(0)
         nc.scalar.copy(
             out=w3_b.rearrange("p (c i j) -> p c j i", i=4, j=PACK),
             in_=w3_raw[:].rearrange("p j (c i) -> p c j i", i=4),
         )
+        fetch(0)
         scatter(2)
         fetch(1)
         for lo, hi in ((0, HALF), (HALF, N)):
             nc.vector.quantize_mx(
                 out=w3_q[:, lo:hi].bitcast(FP8X4), scales=w3_s[:, lo:hi], in_=w3_b[:, PACK * lo : PACK * hi]
             )
-        fetch(2)
+        for c in range(PAGE_CHUNKS):
+            turn_page(2, c)
+        held = {}
+        for h in range(2):
+            for t in (2, 3):
+                held[t, h] = bank(HELD_BANKS[2 * h + t - 2], "xt_bank%d_%d" % (t, h))
+                open_x(held[t, h], t)
         scatter(3)
+        picked[0] = sb.tile([P, S], F32, tag="last", bufs=1, name="picked2")
+        for h in range(2):
+            for t in (2, 3):
+                nc.vector.tensor_copy(
+                    out=picked[t % 2][:, HALF * h : HALF * (h + 1)], in_=page[t][:].indirect(list3[:, 32 * h : 32 * (h + 1)])
+                )
 
-        t = PACK - 1
-        x_q = sb.tile([P, S], U32, name="x_q", align_bytes=64)
+        x_q = sb.tile([P, S], U32, tag="raw3", name="x_q", align_bytes=64)
         x_s = sb.tile([P, S], U8, name="x_s", align_bytes=64)
-        for h in range(2):
-            slot = picked[:, S + HALF * h : S + HALF * (h + 1)]
-            nc.vector.tensor_copy(out=slot, in_=page[t][:].indirect(list3[:, 32 * h : 32 * (h + 1)]))
-            nc.scalar.activation(out=x_view[:, 1, 1, h], in_=slot, func=ACT.Identity, bias=neg_ref[:, t : t + 1])
-        for h in range(2):
-            span = slice(PACK * HALF * h, PACK * HALF * (h + 1))
-            cols = slice(HALF * h, HALF * (h + 1))
-            nc.vector.tensor_copy(
-                out=x_b[:, span].bitcast(I32).rearrange("p (j u) -> p j u", u=2),
-                in_=x_pairs[:, span].bitcast(I32).rearrange("p (u j) -> p j u", u=2),
-            )
-            nc.vector.quantize_mx(out=x_q[:, cols].bitcast(FP8X4), scales=x_s[:, cols], in_=x_b[:, span])
 
-        p_q = sb.tile([P, T2], U32, tag="raw2", name="p_q", align_bytes=64)
+        def quantise_x(h):
+            cols = slice(HALF * h, HALF * (h + 1))
+            x_half = x_b[:, PACK * HALF * h : PACK * HALF * (h + 1)]
+            for t in (2, 3):
+                close_x(held[t, h], t, h)
+            ring.extend(HELD_BANKS[2 * h : 2 * h + 2])
+            for half in range(2):
+                turn_back(x_turned, h, half, x_half, half == 1, "xb_bank%d_%d" % (h, half))
+            nc.vector.quantize_mx(out=x_q[:, cols].bitcast(FP8X4), scales=x_s[:, cols], in_=x_half)
+
+        p_q = sb.tile([P, T2], U32, name="p_q", align_bytes=64)
         p_s = sb.tile([P, T2], U8, name="p_s", align_bytes=64)
         words_out = out_2[0].rearrange("p m t -> p (m t)").bitcast(I32)
 
         def planes(c):
             cols = slice(HALF * c, HALF * (c + 1))
-            span = slice(PACK * HALF * c, PACK * HALF * (c + 1))
-            nc.scalar.copy(out=p_view[:, 1, 1, c], in_=page[t][:, cols])
             p_b = sb.tile([P, PACK * HALF], BF16, tag="stage", bufs=2, name="p_b%d" % c, align_bytes=64)
-            if c in SCALAR_WEAVES:
-                nc.scalar.copy(
-                    out=p_b[:].bitcast(U32).rearrange("p (m u) -> p m u", u=2),
-                    in_=p_pairs[:, span].bitcast(U32).rearrange("p (u m) -> p m u", u=2),
-                )
-            else:
-                nc.vector.tensor_copy(
-                    out=p_b[:].bitcast(I32).rearrange("p (m u) -> p m u", u=2),
-                    in_=p_pairs[:, span].bitcast(I32).rearrange("p (u m) -> p m u", u=2),
-                )
+            for half in range(2):
+                turn_back(p_turned, c, half, p_b[:], (c, half) in VECTOR_TURNS, "pb_bank%d_%d" % (c, half))
             nc.vector.quantize_mx(out=p_q[:, cols].bitcast(FP8X4), scales=p_s[:, cols], in_=p_b[:])
             nc.sync.dma_start(out=words_out[:, cols], in_=p_q[:, cols].bitcast(I32))
 
@@ -324,25 +352,32 @@ def tile_list_flue_liner_page_kernel(
             h, nt = divmod(i, N // P)
             cols = slice(HALF * h, HALF * (h + 1))
             rows = slice(P * nt, P * (nt + 1))
-            e_bank = bank((2 * i) % 8, "e_bank%d" % i)
-            f_bank = bank((2 * i + 1) % 8, "f_bank%d" % i)
+            e_bank = next_bank("e_bank%d" % i)
+            f_bank = next_bank("f_bank%d" % i)
             for acc, words, scales in ((e_bank, w3_q, w3_s), (f_bank, w4_w, w4_s)):
                 nc.tensor.matmul_mx(
                     out=acc[:], lhsT=words[:, rows].bitcast(FP8X4), lhsT_scale=scales[:, rows],
                     rhs=x_q[:, cols].bitcast(FP8X4), rhs_scale=x_s[:, cols], start=True, stop=True,
                 )
-            gel = sb.tile([P, HALF], F32, tag="small", bufs=3, name="gel%d" % i)
+            gel = sb.tile([P, HALF], F32, tag="abs", bufs=3, name="gel%d" % i)
             nc.scalar.activation(out=gel[:], in_=e_bank[:], func=ACT.Gelu_apprx_tanh)
-            y = sb.tile([P, HALF], F32, tag=("mid", "gain")[i % 2], bufs=4, name="y%d" % i)
+            tag, bufs = (("more", 4), ("mid", 3))[i % 2]
+            y = sb.tile([P, HALF], F32, tag=tag, bufs=bufs, name="y%d" % i)
             nc.vector.tensor_tensor(out=y[:], in0=f_bank[:], in1=gel[:], op=ALU.add)
             nc.sync.dma_start(out=out_0[rows, cols], in_=y[:])
 
+        for c in range(PAGE_CHUNKS - 1):
+            turn_page(PACK - 1, c)
         planes(0)
+        quantise_x(0)
+        turn_page(PACK - 1, PAGE_CHUNKS - 1)
+        planes(1)
+        quantise_x(1)
         for i in range(2 * (N // P)):
             second_stage(i)
-            if i in (1, 3, 5):
-                planes((i + 1) // 2)
-            if i == 5:
+            if i in (1, 3):
+                planes((i + 3) // 2)
+            if i == 3:
                 for q in range(QUADS):
                     nc.sync.dma_start(
                         out=out_3[0, 4 * q : 4 * q + 4, :].bitcast(I32), in_=p_s[32 * q : 32 * q + 4, :].bitcast(I32)

@@ -126,6 +126,8 @@ def tile_list_flue_liner_page_kernel(
         load_w4_scales(0, QUADS)
 
         make_identity(nc, ident[:])
+        unread = sb.tile([P, 1], F32, name="unread")
+        nc.scalar.activation(out=unread[:], in_=ident[:, 0:1], func=ACT.Gelu_apprx_tanh)
         ref_bank = bank(7, "ref_bank")
         nc.tensor.transpose(ref_bank[:, 0:P], ref_rows[:], ident[:])
         nc.scalar.activation(out=neg_ref[:], in_=ref_bank[:, 0:PACK], func=ACT.Copy, scale=-1.0)

from contextlib import ExitStack

import concourse.mybir as mybir
from concourse.masks import make_identity

F32 = mybir.dt.float32
BF16 = mybir.dt.bfloat16
I32 = mybir.dt.int32
U32 = mybir.dt.uint32
U16 = mybir.dt.uint16
U8 = mybir.dt.uint8
FP8X4 = mybir.dt.float8_e4m3fn_x4
FP4X4 = mybir.dt.float4_e2m1fn_x4
ACT = mybir.ActivationFunctionType
ALU = mybir.AluOpType

FLOPS = 4563402752

P = 128
PACK = 4
PASSES = 3
H = 512
N = 640
T = 4096
S = 1024
T2 = 2048
HALF = 512
QUADS = 4
A_BANKS = (0, 2, 3, 4, 6, 7)
D_BANKS = (1, 5)
PAGE_CHUNKS = 4
VECTOR_TURNS = ((1, 1), (3, 1))
LATE_BANKS = (0, 1, 2, 5)
HELD_BANKS = (3, 4, 6, 7)


def tile_list_flue_liner_page_kernel(
    tc, tab_words, tab_scales, offs, offs2, offs3, w1, w2_words, w2_scales, page0, wgs, ref, w3, w4_words, w4_scales,
    out_0, out_1, out_2, out_3,
):
    nc = tc.nc
    with ExitStack() as ctx:
        lists = ctx.enter_context(tc.tile_pool(name="lists", bufs=1))
        sb = ctx.enter_context(tc.tile_pool(name="sb", bufs=1))
        psum = ctx.enter_context(tc.psum_pool(name="psum", bufs=1))

        def bank(i, name):
            return psum.tile([P, HALF], F32, tag="bank%d" % i, name=name)

        list1 = lists.tile([P, S // 16], U16, name="list1")
        list2 = lists.tile([P, S // 16], U16, name="list2")
        list3 = lists.tile([P, S // 16], U16, name="list3")

        tab = [sb.tile([P, T], U32, name="tab%d" % a, align_bytes=64) for a in range(PASSES)]
        tab_sc = sb.tile([P, T], U8, name="tab_sc", align_bytes=64)
        w2_w = sb.tile([P, PASSES, 2 * H], U8, name="w2_w", align_bytes=64)
        w2_s = sb.tile([P, PASSES, H], U8, name="w2_s", align_bytes=64)
        w4_w = sb.tile([P, N], U32, name="w4_w", align_bytes=64)
        w4_s = sb.tile([P, N], U8, name="w4_s", align_bytes=64)
        v_sc = sb.tile([P, S], U8, name="v_sc", align_bytes=64)
        v_planes = sb.tile([P, PASSES, S], U8, name="v_planes", align_bytes=64)
        w1_raw = [sb.tile([P, PACK, H], F32, tag="raw%d" % a, name="w1_raw%d" % a, align_bytes=64) for a in range(PASSES)]
        w3_raw = sb.tile([P, PACK, N], F32, tag="raw3", name="w3_raw", align_bytes=64)
        page = [sb.tile([P, T2], F32, name="page%d" % t) for t in range(PACK)]
        gain = sb.tile([P, S], F32, name="gain")
        ref_rows = sb.tile([P, P], F32, name="ref_rows")
        neg_ref = sb.tile([P, PACK], F32, name="neg_ref")
        ident = sb.tile([P, P], F32, name="ident")

        nc.vector.memset(tab_sc[:].bitcast(I32), 0)
        nc.vector.memset(w2_s[:].rearrange("p a c -> p (a c)").bitcast(I32), 0)
        nc.vector.memset(v_planes[:].rearrange("p a j -> p (a j)").bitcast(I32), 0)
        nc.vector.memset(w4_s[:].bitcast(I32), 0)
        nc.gpsimd.memset(ref_rows[:], 0.0)

        def load_tab(a, cols=slice(0, T)):
            words = tab_words[a].rearrange("p t i -> p (t i)").bitcast(I32)
            nc.sync.dma_start(out=tab[a][:, cols].bitcast(I32), in_=words[:, cols])

        def load_w4_scales(lo, hi):
            for q in range(lo, hi):
                nc.sync.dma_start(
                    out=w4_s[32 * q : 32 * q + 4, :].bitcast(I32), in_=w4_scales[0, 4 * q : 4 * q + 4, :].bitcast(I32)
                )

        page_in = page0.rearrange("(t p) m -> t p m", p=P)
        page_out = out_1.rearrange("(t p) m -> t p m", p=P)

        nc.sync.dma_start(list1[:], offs)
        nc.sync.dma_start(list2[:], offs2)
        nc.sync.dma_start(list3[:], offs3)
        load_tab(0, slice(0, T // 2))
        load_tab(0, slice(T // 2, T))
        w2_in = w2_words.rearrange("a p b -> p a b").bitcast(I32)
        for a in range(PASSES):
            nc.sync.dma_start(out=w2_w[:, a].bitcast(I32), in_=w2_in[:, a])
        nc.sync.dma_start(
            out=tab_sc[0 : 16 * PASSES, :].bitcast(I32), in_=tab_scales.rearrange("a q t -> q a t").bitcast(I32)
        )
        load_tab(1, slice(0, T // 2))
        load_tab(1, slice(T // 2, 3 * T // 4))
        load_tab(1, slice(3 * T // 4, T))
        for q in range(QUADS):
            nc.sync.dma_start(
                out=w2_s[32 * q : 32 * q + 4].bitcast(I32),
                in_=w2_scales[:, 4 * q : 4 * q + 4, :].rearrange("a r c -> r a c").bitcast(I32),
            )
        nc.sync.dma_start(out=ref_rows[0:PACK, :], in_=ref.rearrange("(t p) -> t p", p=P))
        load_tab(2)
        nc.vector.tensor_copy(out=v_sc[:], in_=tab_sc[:].indirect(list1[:]))
        for q in range(QUADS):
            nc.sync.dma_start(
                out=v_planes[32 * q : 32 * q + 4].bitcast(I32),
                in_=v_sc[4 * PASSES * q : 4 * PASSES * (q + 1), :].bitcast(I32),
            )
        for a in range(PASSES):
            nc.sync.dma_start(out=w1_raw[a][:], in_=w1[H * a : H * (a + 1), :].rearrange("(p j) c -> p j c", j=PACK))
        nc.sync.dma_start(out=gain[:, 0:HALF], in_=wgs[:, 0:HALF])
        nc.sync.dma_start(out=page[0][:], in_=page_in[0])
        nc.sync.dma_start(out=gain[:, HALF:S], in_=wgs[:, HALF:S])
        nc.sync.dma_start(out=page[1][:], in_=page_in[1])
        nc.sync.dma_start(out=w3_raw[:], in_=w3.rearrange("(p j) n -> p j n", j=PACK))
        nc.sync.dma_start(out=page[2][:], in_=page_in[2])
        nc.sync.dma_start(out=page[3][:], in_=page_in[3])
        nc.sync.dma_start(out=w4_w[:].bitcast(I32), in_=w4_words[0].rearrange("p c i -> p (c i)").bitcast(I32))
        load_w4_scales(0, QUADS)

        make_identity(nc, ident[:])
        unread = sb.tile([P, 1], F32, name="unread")
        nc.scalar.activation(out=unread[:], in_=ident[:, 0:1], func=ACT.Gelu_apprx_tanh)
        ref_bank = bank(7, "ref_bank")
        nc.tensor.transpose(ref_bank[:, 0:P], ref_rows[:], ident[:])
        nc.scalar.activation(out=neg_ref[:], in_=ref_bank[:, 0:PACK], func=ACT.Copy, scale=-1.0)
        v_w = [sb.tile([P, S], U32, name="v_w%d" % a, align_bytes=64) for a in range(PASSES)]
        blocks = S // P
        b_bank = [bank(jb, "b_bank%d" % jb) for jb in range(blocks)]
        neg_b = sb.tile([P, blocks * H], F32, tag="big", name="neg_b", align_bytes=64)
        for a in range(PASSES):
            pieces = 2 if a == PASSES - 1 else 1
            for h in range(pieces):
                n = S // pieces
                nc.vector.tensor_copy(
                    out=v_w[a][:, n * h : n * (h + 1)], in_=tab[a][:].indirect(list1[:, n // 16 * h : n // 16 * (h + 1)])
                )

        def b_pass(jb, a):
            cols = slice(P * jb, P * (jb + 1))
            nc.tensor.matmul_mx(
                out=b_bank[jb][:],
                lhsT=v_w[a][:, cols].bitcast(FP8X4),
                lhsT_scale=v_planes[:, a, cols],
                rhs=w2_w[:, a, :].bitcast(FP4X4),
                rhs_scale=w2_s[:, a, :],
                start=(a == 0),
                stop=(a == PASSES - 1),
            )

        for jb in range(blocks):
            for a in range(PASSES):
                b_pass(jb, a)

        def negate_b(h):
            for jb in range(4 * h, 4 * h + 4):
                nc.scalar.activation(out=neg_b[:, H * jb : H * (jb + 1)], in_=b_bank[jb][:], func=ACT.Copy, scale=-1.0)

        negate_b(0)

        w1_q = [sb.tile([P, H], U32, name="w1_q%d" % a, align_bytes=64) for a in range(PASSES)]
        w1_s = [sb.tile([P, H], U8, name="w1_s%d" % a, align_bytes=64) for a in range(PASSES)]
        last = PASSES - 1

        for a in range(PASSES):
            staged = sb.tile([P, PACK * H], BF16, tag="stage", bufs=2, name="w1_b%d" % a, align_bytes=64)
            width = P if a == last else H
            for lo in range(0, H, width):
                rounded_cols = staged[:, PACK * lo : PACK * (lo + width)]
                nc.vector.tensor_copy(
                    out=rounded_cols.rearrange("p (c i j) -> p c j i", i=4, j=PACK),
                    in_=w1_raw[a][:, :, lo : lo + width].rearrange("p j (c i) -> p c j i", i=4),
                )
                nc.vector.quantize_mx(
                    out=w1_q[a][:, lo : lo + width].bitcast(FP8X4), scales=w1_s[a][:, lo : lo + width], in_=rounded_cols
                )

        def add_turned(acc, parts, opens):
            for i, block in enumerate(parts):
                nc.tensor.matmul(
                    acc[:, P * i : P * (i + 1)], lhsT=block, rhs=ident[:], is_transpose=True,
                    start=(opens and i == 0), stop=(not opens and i == 3),
                )

        groups = 2 * PACK
        a_bank = {}

        def a_pass(g, a):
            t, h = divmod(g, 2)
            if a == 0:
                a_bank[g] = bank(A_BANKS[g % len(A_BANKS)], "a_bank%d" % g)
            for i in range(4):
                cols = slice(HALF * h + P * i, HALF * h + P * (i + 1))
                nc.tensor.matmul_mx(
                    out=a_bank[g][:, P * i : P * (i + 1)],
                    lhsT=v_w[a][:, cols].bitcast(FP8X4),
                    lhsT_scale=v_planes[:, a, cols],
                    rhs=w1_q[a][:, P * t : P * (t + 1)].bitcast(FP8X4),
                    rhs_scale=w1_s[a][:, P * t : P * (t + 1)],
                    start=(a == 0 and i == 0),
                    stop=(a == last and i == 3),
                )

        dev = []
        for g in range(groups):
            t, h = divmod(g, 2)
            if g == 1:
                negate_b(1)
            for a in range(PASSES):
                a_pass(g, a)
            abs_a = sb.tile([P, HALF], F32, tag="abs", bufs=3, name="abs_a%d" % g)
            nc.scalar.activation(out=abs_a[:], in_=a_bank[g][:], func=ACT.Abs)
            d_bank = bank(D_BANKS[g % 2], "d_bank%d" % g)
            first = [neg_b[:, H * (4 * h + i) + P * t : H * (4 * h + i) + P * (t + 1)] for i in range(4)]
            add_turned(d_bank, first, True)
            add_turned(d_bank, [abs_a[:, P * i : P * (i + 1)] for i in range(4)], False)
            if h == 0:
                tag, bufs = ("last", 1) if t == PACK - 1 else ("mid", 3)
                dev.append(sb.tile([P, S], F32, tag=tag, bufs=bufs, name="dev%d" % t))
            nc.scalar.activation(out=dev[t][:, HALF * h : HALF * (h + 1)], in_=d_bank[:], func=ACT.Abs)

        picked = [sb.tile([P, S], F32, tag="raw%d" % n, name="picked%d" % n, align_bytes=64) for n in range(2)]
        x_b = sb.tile([P, PACK * S], BF16, tag="raw2", name="x_b", align_bytes=64)
        rounded = sb.tile([P, PACK * (T2 + S + N)], BF16, tag="big", name="rounded", align_bytes=64)
        p_turned = rounded[:, 0 : PACK * T2]
        x_turned = rounded[:, PACK * T2 : PACK * (T2 + S)]
        w3_b = rounded[:, PACK * (T2 + S) :]
        ring = list(LATE_BANKS)

        def next_bank(name):
            n = ring.pop(0)
            ring.append(n)
            return bank(n, name)

        def scatter(t):
            if t == 0:
                for h in range(2):
                    cols = slice(HALF * h, HALF * (h + 1))
                    nc.vector.tensor_tensor(
                        out=page[t][:].indirect(list2[:, 32 * h : 32 * (h + 1)]),
                        in0=dev[t][:, cols], in1=gain[:, cols], op=ALU.mult,
                    )
            else:
                nc.vector.tensor_tensor(out=page[t][:].indirect(list2[:]), in0=dev[t][:], in1=gain[:], op=ALU.mult)
            nc.sync.dma_start(out=page_out[t], in_=page[t][:])

        def round_out(acc, turned, c, t):
            view = turned[:, PACK * HALF * c : PACK * HALF * (c + 1)].rearrange("m (k u t w) -> m t k u w", k=4, u=2, t=PACK)
            nc.scalar.copy(
                out=view[:, t].rearrange("m k u (q e) -> m k u q e", e=2),
                in_=acc[:].rearrange("m (k q u e) -> m k u q e", k=4, u=2, e=2),
            )

        def turn_page(t, c):
            acc = next_bank("pt_bank%d_%d" % (t, c))
            for i in range(4):
                col = HALF * c + P * i
                nc.tensor.transpose(acc[:, P * i : P * (i + 1)], page[t][:, col : col + P], ident[:])
            round_out(acc, p_turned, c, t)

        def open_x(acc, t):
            add_turned(acc, [neg_ref[:, t : t + 1].to_broadcast([P, P])] * 4, True)

        def close_x(acc, t, h):
            col = HALF * h
            add_turned(acc, [picked[t % 2][:, col + P * i : col + P * (i + 1)] for i in range(4)], False)
            round_out(acc, x_turned, h, t)

        def turn_back(turned, c, half, dst, on_vector, name):
            acc = next_bank(name)
            words = turned[:, PACK * HALF * c + 2 * HALF * half : PACK * HALF * c + 2 * HALF * (half + 1)].bitcast(F32)
            for i in range(4):
                nc.tensor.transpose(acc[:, P * i : P * (i + 1)], words[:, P * i : P * (i + 1)], ident[:])
            out = dst[:, 2 * HALF * half : 2 * HALF * (half + 1)].bitcast(F32).rearrange("p (k m u) -> p k m u", k=2, u=2)
            src = acc[:].rearrange("p (k u m) -> p k m u", k=2, u=2)
            if on_vector:
                nc.vector.tensor_copy(out=out, in_=src)
            else:
                nc.scalar.copy(out=out, in_=src)

        def fetch(t):
            nc.vector.tensor_copy(out=picked[t % 2][:], in_=page[t][:].indirect(list3[:]))
            for c in range(PAGE_CHUNKS):
                turn_page(t, c)
            for h in range(2):
                acc = next_bank("xt_bank%d_%d" % (t, h))
                open_x(acc, t)
                close_x(acc, t, h)

        w3_q = sb.tile([P, N], U32, name="w3_q", align_bytes=64)
        w3_s = sb.tile([P, N], U8, name="w3_s", align_bytes=64)

        scatter(0)
        scatter(1)
        nc.scalar.copy(
            out=w3_b.rearrange("p (c i j) -> p c j i", i=4, j=PACK),
            in_=w3_raw[:].rearrange("p j (c i) -> p c j i", i=4),
        )
        fetch(0)
        scatter(2)
        fetch(1)
        for lo, hi in ((0, HALF), (HALF, N)):
            nc.vector.quantize_mx(
                out=w3_q[:, lo:hi].bitcast(FP8X4), scales=w3_s[:, lo:hi], in_=w3_b[:, PACK * lo : PACK * hi]
            )
        for c in range(PAGE_CHUNKS):
            turn_page(2, c)
        held = {}
        for h in range(2):
            for t in (2, 3):
                held[t, h] = bank(HELD_BANKS[2 * h + t - 2], "xt_bank%d_%d" % (t, h))
                open_x(held[t, h], t)
        scatter(3)
        picked[0] = sb.tile([P, S], F32, tag="last", bufs=1, name="picked2")
        for h in range(2):
            for t in (2, 3):
                nc.vector.tensor_copy(
                    out=picked[t % 2][:, HALF * h : HALF * (h + 1)], in_=page[t][:].indirect(list3[:, 32 * h : 32 * (h + 1)])
                )

        x_q = sb.tile([P, S], U32, tag="raw3", name="x_q", align_bytes=64)
        x_s = sb.tile([P, S], U8, name="x_s", align_bytes=64)

        def quantise_x(h):
            cols = slice(HALF * h, HALF * (h + 1))
            x_half = x_b[:, PACK * HALF * h : PACK * HALF * (h + 1)]
            for t in (2, 3):
                close_x(held[t, h], t, h)
            ring.extend(HELD_BANKS[2 * h : 2 * h + 2])
            for half in range(2):
                turn_back(x_turned, h, half, x_half, half == 1, "xb_bank%d_%d" % (h, half))
            nc.vector.quantize_mx(out=x_q[:, cols].bitcast(FP8X4), scales=x_s[:, cols], in_=x_half)

        p_q = sb.tile([P, T2], U32, name="p_q", align_bytes=64)
        p_s = sb.tile([P, T2], U8, name="p_s", align_bytes=64)
        words_out = out_2[0].rearrange("p m t -> p (m t)").bitcast(I32)

        def planes(c):
            cols = slice(HALF * c, HALF * (c + 1))
            p_b = sb.tile([P, PACK * HALF], BF16, tag="stage", bufs=2, name="p_b%d" % c, align_bytes=64)
            for half in range(2):
                turn_back(p_turned, c, half, p_b[:], (c, half) in VECTOR_TURNS, "pb_bank%d_%d" % (c, half))
            nc.vector.quantize_mx(out=p_q[:, cols].bitcast(FP8X4), scales=p_s[:, cols], in_=p_b[:])
            nc.sync.dma_start(out=words_out[:, cols], in_=p_q[:, cols].bitcast(I32))

        def second_stage(i):
            h, nt = divmod(i, N // P)
            cols = slice(HALF * h, HALF * (h + 1))
            rows = slice(P * nt, P * (nt + 1))
            e_bank = next_bank("e_bank%d" % i)
            f_bank = next_bank("f_bank%d" % i)
            for acc, words, scales in ((e_bank, w3_q, w3_s), (f_bank, w4_w, w4_s)):
                nc.tensor.matmul_mx(
                    out=acc[:], lhsT=words[:, rows].bitcast(FP8X4), lhsT_scale=scales[:, rows],
                    rhs=x_q[:, cols].bitcast(FP8X4), rhs_scale=x_s[:, cols], start=True, stop=True,
                )
            gel = sb.tile([P, HALF], F32, tag="abs", bufs=3, name="gel%d" % i)
            nc.scalar.activation(out=gel[:], in_=e_bank[:], func=ACT.Gelu_apprx_tanh)
            tag, bufs = (("more", 4), ("mid", 3))[i % 2]
            y = sb.tile([P, HALF], F32, tag=tag, bufs=bufs, name="y%d" % i)
            nc.vector.tensor_tensor(out=y[:], in0=f_bank[:], in1=gel[:], op=ALU.add)
            nc.sync.dma_start(out=out_0[rows, cols], in_=y[:])

        for c in range(PAGE_CHUNKS - 1):
            turn_page(PACK - 1, c)
        planes(0)
        quantise_x(0)
        turn_page(PACK - 1, PAGE_CHUNKS - 1)
        planes(1)
        quantise_x(1)
        for i in range(2 * (N // P)):
            second_stage(i)
            if i in (1, 3):
                planes((i + 3) // 2)
            if i == 3:
                for q in range(QUADS):
                    nc.sync.dma_start(
                        out=out_3[0, 4 * q : 4 * q + 4, :].bitcast(I32), in_=p_s[32 * q : 32 * q + 4, :].bitcast(I32)
                    )
